import numpy as np
import ml_dtypes


def mxq(x, axis, fmt="e4m3"):
    dtype, down = {"e4m3": (ml_dtypes.float8_e4m3fn, 7), "e5m2": (ml_dtypes.float8_e5m2, 14)}[fmt]
    v = np.moveaxis(np.asarray(x, np.float32).astype(ml_dtypes.bfloat16).astype(np.float64), axis, -1)
    blocks = v.reshape(v.shape[:-1] + (-1, 32))
    amax = np.abs(blocks).max(-1, keepdims=True)
    byte = np.maximum(np.where(amax > 0, np.frexp(amax)[1] - 1 + 127, 0) - down, 1)
    scale = np.exp2(byte - 127.0)
    codes = (blocks / scale).astype(np.float32).astype(dtype).astype(np.float64)
    return np.moveaxis((codes * scale).reshape(v.shape), -1, axis)


WIDE = False


def mx_kscale(k):
    if not WIDE:
        return np.ones(k)
    levels = np.array([30, -30])
    if k % 512:
        return np.exp2(np.random.permutation(np.resize(levels, k // 32))).repeat(32)
    a = np.empty((k // 512, 16))
    for p in range(k // 512):
        a[p, :8] = np.random.permutation(np.resize(levels, 8))
        for g in range(8):
            far = levels[np.abs(levels - a[p, g]) >= 10]
            a[p, g + 8] = far[np.random.randint(len(far))]
    return np.exp2(a.ravel()).repeat(32)


def f64(x):
    return np.asarray(x).astype(np.float64)


def striped(idx):
    return np.tile(np.asarray(idx).reshape(-1, 16).T, (8, 1)).astype(np.uint16)


def unstriped(offs):
    return offs[:16].T.reshape(-1).astype(np.int64)


E2M1 = np.array([0.0, 0.5, 1.0, 1.5, 2.0, 3.0, 4.0, 6.0, -0.0, -0.5, -1.0, -1.5, -2.0, -3.0, -4.0, -6.0])


def pack_weight(w, fmt):
    k, n = w.shape
    w = f64(np.asarray(w, np.float32).astype(ml_dtypes.bfloat16)).reshape(k // 32, 32, n)
    amax = np.abs(w).max(1)
    if fmt in ("e4m3", "e5m2"):
        byte = np.frexp(amax)[1] - 1 + 127 - (7 if fmt == "e4m3" else 14)
    else:
        mant, ex = np.frexp(amax / 6.0)
        byte = np.where(mant > 0.5, ex, ex - 1) + 127
    byte = np.clip(np.where(amax > 0, byte, 1), 1, 254)
    scaled = (w * np.exp2(127.0 - byte)[:, None, :]).reshape(k, n).astype(np.float32)
    by_word = np.ascontiguousarray(scaled.reshape(k // 512, 128, 4, n).transpose(0, 1, 3, 2))
    if fmt in ("e4m3", "e5m2"):
        words = by_word.astype(ml_dtypes.float8_e4m3fn if fmt == "e4m3" else ml_dtypes.float8_e5m2).view(np.uint8)
    else:
        c = by_word.astype(ml_dtypes.float4_e2m1fn).view(np.uint8) & 0xF
        words = (c[..., 0::2] | (c[..., 1::2] << 4)).reshape(k // 512, 128, 2 * n)
    return np.ascontiguousarray(words), np.ascontiguousarray(byte.astype(np.uint8).reshape(k // 512, 16, n))


def unpack_weight(words, scales, fmt):
    g, _, n = scales.shape
    words = np.ascontiguousarray(words).reshape(g, 128, n, -1)
    if fmt in ("e4m3", "e5m2"):
        vals = words.view(ml_dtypes.float8_e4m3fn if fmt == "e4m3" else ml_dtypes.float8_e5m2).astype(np.float64)
    else:
        nib = np.empty((g, 128, n, 4), np.uint8)
        nib[..., 0::2] = words & 0xF
        nib[..., 1::2] = words >> 4
        vals = E2M1[nib]
    vals = vals * np.repeat(np.exp2(scales.astype(np.float64) - 127.0), 8, axis=1)[..., None]
    return vals.transpose(0, 1, 3, 2).reshape(g * 512, n)


K, T, J, R, O, N, Z = 512, 512, 256, 512, 128, 256, 512


def setup_inputs():
    n = np.random.standard_normal
    idx = np.random.permutation(T)[:J]
    idx2 = np.random.permutation(J)[:O]
    idx3 = np.random.permutation(J)[:O]
    idx4 = np.random.permutation(Z)[:O]
    fk = mx_kscale(K)
    fr = mx_kscale(R)
    xtp = pack_weight(n((K, T)) / fk[:, None], "e5m2")
    wp = pack_weight(n((K, R)) * 1 / np.sqrt(K) * fk[:, None] * fr, "e2m1")
    wbp = pack_weight(n((R, N)) * 1 / np.sqrt(R) / fr[:, None], "e4m3")
    return {
        "xt_words": xtp[0],
        "xt_scales": xtp[1],
        "w_words": wp[0],
        "w_scales": wp[1],
        "wb_words": wbp[0],
        "wb_scales": wbp[1],
        "tz": (n((N, Z)) * 0.6).astype(np.float32),
        "rw": (np.random.uniform(0.5, 2.0, (1, O))).astype(np.float32),
        "offs": striped(idx),
        "offs2": striped(idx2),
        "offs3": striped(idx3),
        "offs4": striped(idx4),
    }


def reference(xt_words, xt_scales, w_words, w_scales, wb_words, wb_scales, tz, rw, offs, offs2, offs3, offs4):
    idx = unstriped(offs)
    idx2 = unstriped(offs2)
    idx3 = unstriped(offs3)
    idx4 = unstriped(offs4)
    xtu = unpack_weight(xt_words, xt_scales, "e5m2")
    wu = unpack_weight(w_words, w_scales, "e2m1")
    wbu = unpack_weight(wb_words, wb_scales, "e4m3")
    xtidxg = xtu[:, idx]
    a = wu.T @ xtidxg
    hid = np.maximum(a[:, idx2], a[:, idx3])
    hidq = mxq(hid, 0, "e5m2")
    p = wbu.T @ hidq
    y = np.maximum(p, f64(tz)[:, idx4]) * f64(rw)
    return y

@@ -1,0 +1,137 @@
+from contextlib import ExitStack
+
+import concourse.mybir as mybir
+
+K, T, J, R, O, N, Z = 512, 512, 256, 512, 128, 256, 512
+FLOPS = 2 * K * R * J + 2 * R * N * O
+
+F32 = mybir.dt.float32
+BF16 = mybir.dt.bfloat16
+I32 = mybir.dt.int32
+U32 = mybir.dt.uint32
+U16 = mybir.dt.uint16
+U8 = mybir.dt.uint8
+E5M2 = mybir.dt.float8_e5m2_x4
+E4M3 = mybir.dt.float8_e4m3fn_x4
+E2M1 = mybir.dt.float4_e2m1fn_x4
+MAX = mybir.AluOpType.max
+MULT = mybir.AluOpType.mult
+COPY = mybir.ActivationFunctionType.Copy
+
+P = 128
+PACK = 4
+
+
+def tile_list_looks_picked_larger_floored_kernel(
+    tc, xt_words, xt_scales, w_words, w_scales, wb_words, wb_scales, tz, rw, offs, offs2, offs3, offs4, out
+):
+    nc = tc.nc
+    with ExitStack() as ctx:
+        keep = ctx.enter_context(tc.tile_pool(name="keep", bufs=1))
+        psum = ctx.enter_context(tc.psum_pool(name="psum", bufs=1))
+
+        l1 = keep.tile([P, J // 16], U16, name="l1")
+        l2 = keep.tile([P, O // 16], U16, name="l2")
+        l3 = keep.tile([P, O // 16], U16, name="l3")
+        l4 = keep.tile([P, O // 16], U16, name="l4")
+        xw = keep.tile([P, T], I32, name="xw", align_bytes=64)
+        xs = keep.tile([P, T // 4], I32, name="xs", align_bytes=64)
+        ww = keep.tile([P, R // 2], I32, name="ww", align_bytes=64)
+        ws = keep.tile([P, R // 4], I32, name="ws", align_bytes=64)
+        bw = keep.tile([P, N], I32, name="bw", align_bytes=64)
+        bs = keep.tile([P, N // 4], I32, name="bs", align_bytes=64)
+        tzt = [keep.tile([P, Z], F32, name="tz%d" % h, align_bytes=64) for h in range(2)]
+        rwt = keep.tile([P, O], F32, name="rwt", align_bytes=64)
+
+        nc.vector.memset(xs[:], 0)
+        nc.vector.memset(ws[:], 0)
+        nc.vector.memset(bs[:], 0)
+
+        def load_scales(queue, tile, src, q):
+            queue.dma_start(out=tile[32 * q : 32 * q + 4, :], in_=src[0, 4 * q : 4 * q + 4, :].bitcast(I32))
+
+        nc.sync.dma_start(l1[:], offs)
+        nc.sync.dma_start(out=xw[:], in_=xt_words[0].rearrange("p n t -> p (n t)").bitcast(I32))
+        nc.sync.dma_start(out=ww[:], in_=w_words[0].bitcast(I32))
+        for q in range(4):
+            load_scales(nc.scalar, xs, xt_scales, q)
+        for q in range(4):
+            load_scales(nc.sync, ws, w_scales, q)
+        nc.sync.dma_start(l2[:], offs2)
+        nc.sync.dma_start(l3[:], offs3)
+        nc.sync.dma_start(out=bw[:], in_=wb_words[0].rearrange("p n t -> p (n t)").bitcast(I32))
+        for q in range(4):
+            load_scales(nc.sync, bs, wb_scales, q)
+        nc.sync.dma_start(l4[:], offs4)
+        for h in range(2):
+            nc.sync.dma_start(out=tzt[h][:], in_=tz[h * P : (h + 1) * P, :])
+        nc.sync.dma_start(out=rwt[:], in_=rw[0].partition_broadcast(P))
+
+        gs = keep.tile([P, J], U8, name="gs", align_bytes=64)
+        gw = keep.tile([P, J], U32, name="gw", align_bytes=64)
+        wd = keep.tile([P, PACK, P], U16, name="wd", align_bytes=64)
+        sd = keep.tile([P, PACK, P], U8, name="sd", align_bytes=64)
+        nc.vector.tensor_copy(gs[:], xs[:].bitcast(U8).indirect(l1[:]))
+        nc.vector.tensor_copy(wd[:], ww[:].bitcast(U16).rearrange("p (q t) -> p t q", t=PACK))
+        nc.vector.tensor_copy(gw[:], xw[:].bitcast(U32).indirect(l1[:]))
+        nc.vector.tensor_copy(sd[:], ws[:].bitcast(U8).rearrange("p (q t) -> p t q", t=PACK))
+
+        g2 = keep.tile([P, PACK, O], F32, name="g2", align_bytes=64)
+        g3 = keep.tile([P, PACK, O], F32, name="g3", align_bytes=64)
+        a_sb = []
+        for t in range(PACK):
+            acc = psum.tile([P, J], F32, name="acc%d" % t)
+            nc.tensor.matmul_mx(
+                out=acc[:],
+                lhsT=wd[:, t, :].bitcast(E2M1),
+                lhsT_scale=sd[:, t, :],
+                rhs=gw[:].bitcast(E5M2),
+                rhs_scale=gs[:],
+                start=True,
+                stop=True,
+            )
+            a_t = keep.tile([P, J], F32, name="a%d" % t, align_bytes=64)
+            if t % 2 == 0:
+                nc.vector.tensor_copy(a_t[:], acc[:])
+            else:
+                nc.scalar.activation(a_t[:], acc[:], COPY)
+            a_sb.append(a_t)
+        for t in range(PACK):
+            for g, lst in ((g2, l2), (g3, l3)):
+                if t % 2 == 0:
+                    nc.vector.tensor_copy(g[:, t, :], a_sb[t][:].indirect(lst[:]))
+                else:
+                    nc.scalar.activation(g[:, t, :], a_sb[t][:].indirect(lst[:]), COPY)
+
+        hid = keep.tile([P, O, PACK], BF16, name="hid", align_bytes=64)
+        nc.vector.tensor_tensor(
+            hid[:].rearrange("p (c i) t -> p c t i", i=4),
+            g2[:].rearrange("p t (c i) -> p c t i", i=4),
+            g3[:].rearrange("p t (c i) -> p c t i", i=4),
+            MAX,
+        )
+        hw = keep.tile([P, O], U32, name="hw", align_bytes=64)
+        hs = keep.tile([P, O], U8, name="hs", align_bytes=64)
+        nc.vector.quantize_mx(out=hw[:].bitcast(E5M2), scales=hs[:], in_=hid[:].rearrange("p o t -> p (o t)"))
+
+        tzg = keep.tile([P, 2, O], F32, name="tzg", align_bytes=64)
+        for h in range(2):
+            nc.scalar.activation(tzg[:, h, :], tzt[h][:].indirect(l4[:]), COPY)
+
+        big = [keep.tile([P, O], F32, name="big%d" % h, align_bytes=64) for h in range(2)]
+        res = [keep.tile([P, O], F32, name="res%d" % h, align_bytes=64) for h in range(2)]
+        for h in range(2):
+            acc2 = psum.tile([P, O], F32, name="out%d" % h)
+            nc.tensor.matmul_mx(
+                out=acc2[:],
+                lhsT=bw[:, h * P : (h + 1) * P].bitcast(E4M3),
+                lhsT_scale=bs[:].bitcast(U8)[:, h * P : (h + 1) * P],
+                rhs=hw[:].bitcast(E5M2),
+                rhs_scale=hs[:],
+                start=True,
+                stop=True,
+            )
+            nc.vector.tensor_tensor(big[h][:], acc2[:], tzg[:, h, :], MAX)
+        for h in range(2):
+            nc.vector.tensor_tensor(res[h][:], big[h][:], rwt[:], MULT)
+            (nc.sync, nc.scalar)[h].dma_start(out=out[h * P : (h + 1) * P, :], in_=res[h][:])

@@ -1,6 +1,7 @@
 from contextlib import ExitStack
 
 import concourse.mybir as mybir
+from concourse.masks import make_identity
 
 K, T, J, R, O, N, Z = 512, 512, 256, 512, 128, 256, 512
 FLOPS = 2 * K * R * J + 2 * R * N * O
@@ -40,32 +41,39 @@ def tile_list_looks_picked_larger_floored_kernel(
         ws = keep.tile([P, R // 4], I32, name="ws", align_bytes=64)
         bw = keep.tile([P, N], I32, name="bw", align_bytes=64)
         bs = keep.tile([P, N // 4], I32, name="bs", align_bytes=64)
-        tzt = [keep.tile([P, Z], F32, name="tz%d" % h, align_bytes=64) for h in range(2)]
-        rwt = keep.tile([P, O], F32, name="rwt", align_bytes=64)
+        tzt = keep.tile([P, 2, Z], F32, name="tzt", align_bytes=64)
+        rwc = keep.tile([P, 1], F32, name="rwc", align_bytes=64)
+        ident = keep.tile([P, P], F32, name="ident", align_bytes=64)
+        make_identity(nc, ident[:])
 
-        nc.vector.memset(xs[:], 0)
         nc.vector.memset(ws[:], 0)
         nc.vector.memset(bs[:], 0)
 
         def load_scales(queue, tile, src, q):
             queue.dma_start(out=tile[32 * q : 32 * q + 4, :], in_=src[0, 4 * q : 4 * q + 4, :].bitcast(I32))
 
+        def load_scales_all(queue, tile, src, q):
+            rows = src[0, 4 * q : 4 * q + 4, :].bitcast(I32)
+            queue.dma_start(out=tile[32 * q : 32 * q + 32, :], in_=rows.unsqueeze(0).to_broadcast([8, 4, rows.shape[1]]))
+
         nc.sync.dma_start(l1[:], offs)
-        nc.sync.dma_start(out=xw[:], in_=xt_words[0].rearrange("p n t -> p (n t)").bitcast(I32))
-        nc.sync.dma_start(out=ww[:], in_=w_words[0].bitcast(I32))
+        load_scales_all(nc.scalar, xs, xt_scales, 0)
+        load_scales_all(nc.sync, xs, xt_scales, 1)
+        load_scales_all(nc.scalar, xs, xt_scales, 2)
+        load_scales_all(nc.sync, xs, xt_scales, 3)
+        nc.scalar.dma_start(out=ww[:], in_=w_words[0].bitcast(I32))
+        with nc.allow_non_contiguous_dma(reason="one weight a partition"):
+            nc.sync.dma_start(out=rwc[:], in_=rw.rearrange("a o -> o a"))
+        nc.scalar.dma_start(out=xw[:], in_=xt_words[0].rearrange("p n t -> p (n t)").bitcast(I32))
         for q in range(4):
-            load_scales(nc.scalar, xs, xt_scales, q)
-        for q in range(4):
-            load_scales(nc.sync, ws, w_scales, q)
+            load_scales((nc.sync, nc.scalar)[q % 2], ws, w_scales, q)
         nc.sync.dma_start(l2[:], offs2)
         nc.sync.dma_start(l3[:], offs3)
-        nc.sync.dma_start(out=bw[:], in_=wb_words[0].rearrange("p n t -> p (n t)").bitcast(I32))
+        nc.sync.dma_start(l4[:], offs4)
+        nc.sync.dma_start(out=tzt[:], in_=tz.rearrange("(h p) z -> p h z", p=P))
         for q in range(4):
             load_scales(nc.sync, bs, wb_scales, q)
-        nc.sync.dma_start(l4[:], offs4)
-        for h in range(2):
-            nc.sync.dma_start(out=tzt[h][:], in_=tz[h * P : (h + 1) * P, :])
-        nc.sync.dma_start(out=rwt[:], in_=rw[0].partition_broadcast(P))
+        nc.sync.dma_start(out=bw[:], in_=wb_words[0].rearrange("p n t -> p (n t)").bitcast(I32))
 
         gs = keep.tile([P, J], U8, name="gs", align_bytes=64)
         gw = keep.tile([P, J], U32, name="gw", align_bytes=64)
@@ -74,13 +82,16 @@ def tile_list_looks_picked_larger_floored_kernel(
         nc.vector.tensor_copy(gs[:], xs[:].bitcast(U8).indirect(l1[:]))
         nc.vector.tensor_copy(wd[:], ww[:].bitcast(U16).rearrange("p (q t) -> p t q", t=PACK))
         nc.vector.tensor_copy(gw[:], xw[:].bitcast(U32).indirect(l1[:]))
-        nc.vector.tensor_copy(sd[:], ws[:].bitcast(U8).rearrange("p (q t) -> p t q", t=PACK))
+        ws_t = ws[:].bitcast(U8).rearrange("p (q t) -> p t q", t=PACK)
+        nc.vector.tensor_copy(sd[:, 0, :], ws_t[:, 0, :])
+        nc.vector.tensor_copy(sd[:, 1, :], ws_t[:, 1, :])
+        nc.vector.tensor_copy(sd[:, 2:, :], ws_t[:, 2:, :])
 
         g2 = keep.tile([P, PACK, O], F32, name="g2", align_bytes=64)
         g3 = keep.tile([P, PACK, O], F32, name="g3", align_bytes=64)
         a_sb = []
         for t in range(PACK):
-            acc = psum.tile([P, J], F32, name="acc%d" % t)
+            acc = psum.tile([P, J], F32, name="acc%d" % t, tag="acc%d" % t)
             nc.tensor.matmul_mx(
                 out=acc[:],
                 lhsT=wd[:, t, :].bitcast(E2M1),
@@ -90,33 +101,47 @@ def tile_list_looks_picked_larger_floored_kernel(
                 start=True,
                 stop=True,
             )
-            a_t = keep.tile([P, J], F32, name="a%d" % t, align_bytes=64)
-            if t % 2 == 0:
+            a_t = keep.tile([P, J], F32, name="a%d" % t, tag="a%d" % t, align_bytes=64)
+            if t == 0:
                 nc.vector.tensor_copy(a_t[:], acc[:])
             else:
                 nc.scalar.activation(a_t[:], acc[:], COPY)
             a_sb.append(a_t)
-        for t in range(PACK):
+        rwt = psum.tile([P, O], F32, name="rwt", tag="acc3")
+        nc.tensor.transpose(rwt[:], rwc[:].to_broadcast([P, P]), ident[:])
+        half = O // 2
+        for t in range(2):
             for g, lst in ((g2, l2), (g3, l3)):
-                if t % 2 == 0:
-                    nc.vector.tensor_copy(g[:, t, :], a_sb[t][:].indirect(lst[:]))
-                else:
-                    nc.scalar.activation(g[:, t, :], a_sb[t][:].indirect(lst[:]), COPY)
+                nc.vector.tensor_copy(g[:, t, :], a_sb[t][:].indirect(lst[:]))
+        for u in range(2):
+            nc.vector.tensor_copy(g2[:, 2, u * half : (u + 1) * half], a_sb[2][:].indirect(l2[:, 4 * u : 4 * u + 4]))
+        nc.scalar.activation(g3[:, 2, :], a_sb[2][:].indirect(l3[:]), COPY)
+        for u in range(2):
+            for g, lst in ((g2, l2), (g3, l3)):
+                nc.scalar.activation(
+                    g[:, 3, u * half : (u + 1) * half], a_sb[3][:].indirect(lst[:, 4 * u : 4 * u + 4]), COPY
+                )
 
         hid = keep.tile([P, O, PACK], BF16, name="hid", align_bytes=64)
-        nc.vector.tensor_tensor(
-            hid[:].rearrange("p (c i) t -> p c t i", i=4),
-            g2[:].rearrange("p t (c i) -> p c t i", i=4),
-            g3[:].rearrange("p t (c i) -> p c t i", i=4),
-            MAX,
-        )
         hw = keep.tile([P, O], U32, name="hw", align_bytes=64)
         hs = keep.tile([P, O], U8, name="hs", align_bytes=64)
-        nc.vector.quantize_mx(out=hw[:].bitcast(E5M2), scales=hs[:], in_=hid[:].rearrange("p o t -> p (o t)"))
+        for u in range(2):
+            cols = slice(u * half, (u + 1) * half)
+            nc.vector.tensor_tensor(
+                hid[:, cols, :].rearrange("p (c i) t -> p c t i", i=4),
+                g2[:, :, cols].rearrange("p t (c i) -> p c t i", i=4),
+                g3[:, :, cols].rearrange("p t (c i) -> p c t i", i=4),
+                MAX,
+            )
+        for u in range(2):
+            cols = slice(u * half, (u + 1) * half)
+            nc.vector.quantize_mx(
+                out=hw[:, cols].bitcast(E5M2), scales=hs[:, cols], in_=hid[:, cols, :].rearrange("p o t -> p (o t)")
+            )
 
-        tzg = keep.tile([P, 2, O], F32, name="tzg", align_bytes=64)
+        tzg = keep.tile([P, 2, O], F32, name="tzg", tag="a1", align_bytes=64)
         for h in range(2):
-            nc.scalar.activation(tzg[:, h, :], tzt[h][:].indirect(l4[:]), COPY)
+            nc.scalar.activation(tzg[:, h, :], tzt[:, h, :].indirect(l4[:]), COPY)
 
         big = [keep.tile([P, O], F32, name="big%d" % h, align_bytes=64) for h in range(2)]
         res = [keep.tile([P, O], F32, name="res%d" % h, align_bytes=64) for h in range(2)]

@@ -21,6 +21,14 @@ COPY = mybir.ActivationFunctionType.Copy
 
 P = 128
 PACK = 4
+QUADS = 4
+QUAD = P // QUADS
+ROWS = 4
+GROUP = 16
+HALF = O // 2
+N_TILES = N // P
+LINE = 4
+ALIGN = 64
 
 
 def tile_list_looks_picked_larger_floored_kernel(
@@ -31,132 +39,134 @@ def tile_list_looks_picked_larger_floored_kernel(
         keep = ctx.enter_context(tc.tile_pool(name="keep", bufs=1))
         psum = ctx.enter_context(tc.psum_pool(name="psum", bufs=1))
 
-        l1 = keep.tile([P, J // 16], U16, name="l1")
-        l2 = keep.tile([P, O // 16], U16, name="l2")
-        l3 = keep.tile([P, O // 16], U16, name="l3")
-        l4 = keep.tile([P, O // 16], U16, name="l4")
-        xw = keep.tile([P, T], I32, name="xw", align_bytes=64)
-        xs = keep.tile([P, T // 4], I32, name="xs", align_bytes=64)
-        ww = keep.tile([P, R // 2], I32, name="ww", align_bytes=64)
-        ws = keep.tile([P, R // 4], I32, name="ws", align_bytes=64)
-        bw = keep.tile([P, N], I32, name="bw", align_bytes=64)
-        bs = keep.tile([P, N // 4], I32, name="bs", align_bytes=64)
-        tzt = keep.tile([P, 2, Z], F32, name="tzt", align_bytes=64)
-        rwc = keep.tile([P, 1], F32, name="rwc", align_bytes=64)
-        ident = keep.tile([P, P], F32, name="ident", align_bytes=64)
-        make_identity(nc, ident[:])
+        list1 = keep.tile([P, J // GROUP], U16, name="list1")
+        list2 = keep.tile([P, O // GROUP], U16, name="list2")
+        list3 = keep.tile([P, O // GROUP], U16, name="list3")
+        list4 = keep.tile([P, O // GROUP], U16, name="list4")
+        xt_codes = keep.tile([P, T], I32, name="xt_codes", align_bytes=ALIGN)
+        xt_plane = keep.tile([P, T // 4], I32, name="xt_plane", align_bytes=ALIGN)
+        w_codes = keep.tile([P, R // 2], I32, name="w_codes", align_bytes=ALIGN)
+        w_plane = keep.tile([P, R // 4], I32, name="w_plane", align_bytes=ALIGN)
+        wb_codes = keep.tile([P, N], I32, name="wb_codes", align_bytes=ALIGN)
+        wb_plane = keep.tile([P, N // 4], I32, name="wb_plane", align_bytes=ALIGN)
+        tz_sb = keep.tile([P, N_TILES, Z], F32, name="tz_sb", align_bytes=ALIGN)
+        rw_column = keep.tile([P, 1], F32, name="rw_column", align_bytes=ALIGN)
+        identity = keep.tile([P, P], F32, name="identity", align_bytes=ALIGN)
+        make_identity(nc, identity[:])
 
-        nc.vector.memset(ws[:], 0)
-        nc.vector.memset(bs[:], 0)
+        nc.vector.memset(w_plane[:], 0)
+        nc.vector.memset(wb_plane[:], 0)
 
-        def load_scales(queue, tile, src, q):
-            queue.dma_start(out=tile[32 * q : 32 * q + 4, :], in_=src[0, 4 * q : 4 * q + 4, :].bitcast(I32))
+        def load_scale_rows(queue, plane, scales, q):
+            rows = scales[0, ROWS * q : ROWS * (q + 1), :].bitcast(I32)
+            queue.dma_start(out=plane[QUAD * q : QUAD * q + ROWS, :], in_=rows)
 
-        def load_scales_all(queue, tile, src, q):
-            rows = src[0, 4 * q : 4 * q + 4, :].bitcast(I32)
-            queue.dma_start(out=tile[32 * q : 32 * q + 32, :], in_=rows.unsqueeze(0).to_broadcast([8, 4, rows.shape[1]]))
+        def load_scale_rows_repeated(queue, plane, scales, q):
+            rows = scales[0, ROWS * q : ROWS * (q + 1), :].bitcast(I32)
+            repeated = rows.unsqueeze(0).to_broadcast([QUAD // ROWS, ROWS, rows.shape[1]])
+            queue.dma_start(out=plane[QUAD * q : QUAD * (q + 1), :], in_=repeated)
 
-        nc.sync.dma_start(l1[:], offs)
-        load_scales_all(nc.scalar, xs, xt_scales, 0)
-        load_scales_all(nc.sync, xs, xt_scales, 1)
-        load_scales_all(nc.scalar, xs, xt_scales, 2)
-        load_scales_all(nc.sync, xs, xt_scales, 3)
-        nc.scalar.dma_start(out=ww[:], in_=w_words[0].bitcast(I32))
+        nc.sync.dma_start(list1[:], offs)
+        for q in range(QUADS):
+            load_scale_rows_repeated((nc.scalar, nc.sync)[q % 2], xt_plane, xt_scales, q)
+        nc.scalar.dma_start(out=w_codes[:], in_=w_words[0].bitcast(I32))
         with nc.allow_non_contiguous_dma(reason="one weight a partition"):
-            nc.sync.dma_start(out=rwc[:], in_=rw.rearrange("a o -> o a"))
-        nc.scalar.dma_start(out=xw[:], in_=xt_words[0].rearrange("p n t -> p (n t)").bitcast(I32))
-        for q in range(4):
-            load_scales((nc.sync, nc.scalar)[q % 2], ws, w_scales, q)
-        nc.sync.dma_start(l2[:], offs2)
-        nc.sync.dma_start(l3[:], offs3)
-        nc.sync.dma_start(l4[:], offs4)
-        nc.sync.dma_start(out=tzt[:], in_=tz.rearrange("(h p) z -> p h z", p=P))
-        for q in range(4):
-            load_scales(nc.sync, bs, wb_scales, q)
-        nc.sync.dma_start(out=bw[:], in_=wb_words[0].rearrange("p n t -> p (n t)").bitcast(I32))
+            nc.sync.dma_start(out=rw_column[:], in_=rw.rearrange("a o -> o a"))
+        nc.scalar.dma_start(out=xt_codes[:], in_=xt_words[0].rearrange("p n t -> p (n t)").bitcast(I32))
+        for q in range(QUADS):
+            load_scale_rows((nc.sync, nc.scalar)[q % 2], w_plane, w_scales, q)
+        nc.sync.dma_start(list2[:], offs2)
+        nc.sync.dma_start(list3[:], offs3)
+        nc.sync.dma_start(list4[:], offs4)
+        nc.sync.dma_start(out=tz_sb[:], in_=tz.rearrange("(h p) z -> p h z", p=P))
+        for q in range(QUADS):
+            load_scale_rows(nc.sync, wb_plane, wb_scales, q)
+        nc.sync.dma_start(out=wb_codes[:], in_=wb_words[0].rearrange("p n t -> p (n t)").bitcast(I32))
 
-        gs = keep.tile([P, J], U8, name="gs", align_bytes=64)
-        gw = keep.tile([P, J], U32, name="gw", align_bytes=64)
-        wd = keep.tile([P, PACK, P], U16, name="wd", align_bytes=64)
-        sd = keep.tile([P, PACK, P], U8, name="sd", align_bytes=64)
-        nc.vector.tensor_copy(gs[:], xs[:].bitcast(U8).indirect(l1[:]))
-        nc.vector.tensor_copy(wd[:], ww[:].bitcast(U16).rearrange("p (q t) -> p t q", t=PACK))
-        nc.vector.tensor_copy(gw[:], xw[:].bitcast(U32).indirect(l1[:]))
-        ws_t = ws[:].bitcast(U8).rearrange("p (q t) -> p t q", t=PACK)
-        nc.vector.tensor_copy(sd[:, 0, :], ws_t[:, 0, :])
-        nc.vector.tensor_copy(sd[:, 1, :], ws_t[:, 1, :])
-        nc.vector.tensor_copy(sd[:, 2:, :], ws_t[:, 2:, :])
+        picked_plane = keep.tile([P, J], U8, name="picked_plane", align_bytes=ALIGN)
+        picked_codes = keep.tile([P, J], U32, name="picked_codes", align_bytes=ALIGN)
+        dealt_codes = keep.tile([P, PACK, P], U16, name="dealt_codes", align_bytes=ALIGN)
+        dealt_plane = keep.tile([P, PACK, P], U8, name="dealt_plane", align_bytes=ALIGN)
+        nc.vector.tensor_copy(picked_plane[:], xt_plane[:].bitcast(U8).indirect(list1[:]))
+        nc.vector.tensor_copy(dealt_codes[:], w_codes[:].bitcast(U16).rearrange("p (q t) -> p t q", t=PACK))
+        nc.vector.tensor_copy(picked_codes[:], xt_codes[:].bitcast(U32).indirect(list1[:]))
+        w_plane_by_slice = w_plane[:].bitcast(U8).rearrange("p (q t) -> p t q", t=PACK)
+        nc.vector.tensor_copy(dealt_plane[:, 0, :], w_plane_by_slice[:, 0, :])
+        nc.vector.tensor_copy(dealt_plane[:, 1, :], w_plane_by_slice[:, 1, :])
+        nc.vector.tensor_copy(dealt_plane[:, 2:, :], w_plane_by_slice[:, 2:, :])
 
-        g2 = keep.tile([P, PACK, O], F32, name="g2", align_bytes=64)
-        g3 = keep.tile([P, PACK, O], F32, name="g3", align_bytes=64)
-        a_sb = []
+        a_by_list2 = keep.tile([P, PACK, O], F32, name="a_by_list2", align_bytes=ALIGN)
+        a_by_list3 = keep.tile([P, PACK, O], F32, name="a_by_list3", align_bytes=ALIGN)
+        a_slices = []
         for t in range(PACK):
-            acc = psum.tile([P, J], F32, name="acc%d" % t, tag="acc%d" % t)
+            a_bank = psum.tile([P, J], F32, name="a_bank%d" % t, tag="a_bank%d" % t)
             nc.tensor.matmul_mx(
-                out=acc[:],
-                lhsT=wd[:, t, :].bitcast(E2M1),
-                lhsT_scale=sd[:, t, :],
-                rhs=gw[:].bitcast(E5M2),
-                rhs_scale=gs[:],
+                out=a_bank[:],
+                lhsT=dealt_codes[:, t, :].bitcast(E2M1),
+                lhsT_scale=dealt_plane[:, t, :],
+                rhs=picked_codes[:].bitcast(E5M2),
+                rhs_scale=picked_plane[:],
                 start=True,
                 stop=True,
             )
-            a_t = keep.tile([P, J], F32, name="a%d" % t, tag="a%d" % t, align_bytes=64)
+            a_slice = keep.tile([P, J], F32, name="a_slice%d" % t, tag="a_slice%d" % t, align_bytes=ALIGN)
             if t == 0:
-                nc.vector.tensor_copy(a_t[:], acc[:])
+                nc.vector.tensor_copy(a_slice[:], a_bank[:])
             else:
-                nc.scalar.activation(a_t[:], acc[:], COPY)
-            a_sb.append(a_t)
-        rwt = psum.tile([P, O], F32, name="rwt", tag="acc3")
-        nc.tensor.transpose(rwt[:], rwc[:].to_broadcast([P, P]), ident[:])
-        half = O // 2
-        for t in range(2):
-            for g, lst in ((g2, l2), (g3, l3)):
-                nc.vector.tensor_copy(g[:, t, :], a_sb[t][:].indirect(lst[:]))
-        for u in range(2):
-            nc.vector.tensor_copy(g2[:, 2, u * half : (u + 1) * half], a_sb[2][:].indirect(l2[:, 4 * u : 4 * u + 4]))
-        nc.scalar.activation(g3[:, 2, :], a_sb[2][:].indirect(l3[:]), COPY)
-        for u in range(2):
-            for g, lst in ((g2, l2), (g3, l3)):
-                nc.scalar.activation(
-                    g[:, 3, u * half : (u + 1) * half], a_sb[3][:].indirect(lst[:, 4 * u : 4 * u + 4]), COPY
-                )
+                nc.scalar.activation(a_slice[:], a_bank[:], COPY)
+            a_slices.append(a_slice)
 
-        hid = keep.tile([P, O, PACK], BF16, name="hid", align_bytes=64)
-        hw = keep.tile([P, O], U32, name="hw", align_bytes=64)
-        hs = keep.tile([P, O], U8, name="hs", align_bytes=64)
-        for u in range(2):
-            cols = slice(u * half, (u + 1) * half)
+        rw_rows = psum.tile([P, O], F32, name="rw_rows", tag="a_bank%d" % (PACK - 1))
+        nc.tensor.transpose(rw_rows[:], rw_column[:].to_broadcast([P, P]), identity[:])
+
+        looks = ((a_by_list2, list2), (a_by_list3, list3))
+        halves = [(slice(u * HALF, (u + 1) * HALF), slice(u * HALF // GROUP, (u + 1) * HALF // GROUP)) for u in range(2)]
+        for t in (0, 1):
+            for picked, entries in looks:
+                nc.vector.tensor_copy(picked[:, t, :], a_slices[t][:].indirect(entries[:]))
+        for places, columns in halves:
+            nc.vector.tensor_copy(a_by_list2[:, 2, places], a_slices[2][:].indirect(list2[:, columns]))
+        nc.scalar.activation(a_by_list3[:, 2, :], a_slices[2][:].indirect(list3[:]), COPY)
+        for places, columns in halves:
+            for picked, entries in looks:
+                nc.scalar.activation(picked[:, 3, places], a_slices[3][:].indirect(entries[:, columns]), COPY)
+
+        hid = keep.tile([P, O, PACK], BF16, name="hid", align_bytes=ALIGN)
+        hid_codes = keep.tile([P, O], U32, name="hid_codes", align_bytes=ALIGN)
+        hid_plane = keep.tile([P, O], U8, name="hid_plane", align_bytes=ALIGN)
+        for places, columns in halves:
             nc.vector.tensor_tensor(
-                hid[:, cols, :].rearrange("p (c i) t -> p c t i", i=4),
-                g2[:, :, cols].rearrange("p t (c i) -> p c t i", i=4),
-                g3[:, :, cols].rearrange("p t (c i) -> p c t i", i=4),
+                hid[:, places, :].rearrange("p (c i) t -> p c t i", i=LINE),
+                a_by_list2[:, :, places].rearrange("p t (c i) -> p c t i", i=LINE),
+                a_by_list3[:, :, places].rearrange("p t (c i) -> p c t i", i=LINE),
                 MAX,
             )
-        for u in range(2):
-            cols = slice(u * half, (u + 1) * half)
+        for places, columns in halves:
             nc.vector.quantize_mx(
-                out=hw[:, cols].bitcast(E5M2), scales=hs[:, cols], in_=hid[:, cols, :].rearrange("p o t -> p (o t)")
+                out=hid_codes[:, places].bitcast(E5M2),
+                scales=hid_plane[:, places],
+                in_=hid[:, places, :].rearrange("p o t -> p (o t)"),
             )
 
-        tzg = keep.tile([P, 2, O], F32, name="tzg", tag="a1", align_bytes=64)
-        for h in range(2):
-            nc.scalar.activation(tzg[:, h, :], tzt[:, h, :].indirect(l4[:]), COPY)
+        tz_picked = keep.tile([P, N_TILES, O], F32, name="tz_picked", tag="a_slice%d" % (PACK - 1), align_bytes=ALIGN)
+        for h in range(N_TILES):
+            nc.scalar.activation(tz_picked[:, h, :], tz_sb[:, h, :].indirect(list4[:]), COPY)
 
-        big = [keep.tile([P, O], F32, name="big%d" % h, align_bytes=64) for h in range(2)]
-        res = [keep.tile([P, O], F32, name="res%d" % h, align_bytes=64) for h in range(2)]
-        for h in range(2):
-            acc2 = psum.tile([P, O], F32, name="out%d" % h)
+        floored = [keep.tile([P, O], F32, name="floored%d" % h, align_bytes=ALIGN) for h in range(N_TILES)]
+        result = [keep.tile([P, O], F32, name="result%d" % h, align_bytes=ALIGN) for h in range(N_TILES)]
+        for h in range(N_TILES):
+            features = slice(h * P, (h + 1) * P)
+            p_bank = psum.tile([P, O], F32, name="p_bank%d" % h)
             nc.tensor.matmul_mx(
-                out=acc2[:],
-                lhsT=bw[:, h * P : (h + 1) * P].bitcast(E4M3),
-                lhsT_scale=bs[:].bitcast(U8)[:, h * P : (h + 1) * P],
-                rhs=hw[:].bitcast(E5M2),
-                rhs_scale=hs[:],
+                out=p_bank[:],
+                lhsT=wb_codes[:, features].bitcast(E4M3),
+                lhsT_scale=wb_plane[:].bitcast(U8)[:, features],
+                rhs=hid_codes[:].bitcast(E5M2),
+                rhs_scale=hid_plane[:],
                 start=True,
                 stop=True,
             )
-            nc.vector.tensor_tensor(big[h][:], acc2[:], tzg[:, h, :], MAX)
-        for h in range(2):
-            nc.vector.tensor_tensor(res[h][:], big[h][:], rwt[:], MULT)
-            (nc.sync, nc.scalar)[h].dma_start(out=out[h * P : (h + 1) * P, :], in_=res[h][:])
+            nc.vector.tensor_tensor(floored[h][:], p_bank[:], tz_picked[:, h, :], MAX)
+        for h in range(N_TILES):
+            nc.vector.tensor_tensor(result[h][:], floored[h][:], rw_rows[:], MULT)
+            (nc.sync, nc.scalar)[h].dma_start(out=out[h * P : (h + 1) * P, :], in_=result[h][:])

from contextlib import ExitStack

import concourse.mybir as mybir
from concourse.masks import make_identity

K, T, J, R, O, N, Z = 512, 512, 256, 512, 128, 256, 512
FLOPS = 2 * K * R * J + 2 * R * N * O

F32 = mybir.dt.float32
BF16 = mybir.dt.bfloat16
I32 = mybir.dt.int32
U32 = mybir.dt.uint32
U16 = mybir.dt.uint16
U8 = mybir.dt.uint8
E5M2 = mybir.dt.float8_e5m2_x4
E4M3 = mybir.dt.float8_e4m3fn_x4
E2M1 = mybir.dt.float4_e2m1fn_x4
MAX = mybir.AluOpType.max
MULT = mybir.AluOpType.mult
COPY = mybir.ActivationFunctionType.Copy

P = 128
PACK = 4
QUADS = 4
QUAD = P // QUADS
ROWS = 4
GROUP = 16
HALF = O // 2
N_TILES = N // P
LINE = 4
ALIGN = 64


def tile_list_looks_picked_larger_floored_kernel(
    tc, xt_words, xt_scales, w_words, w_scales, wb_words, wb_scales, tz, rw, offs, offs2, offs3, offs4, out
):
    nc = tc.nc
    with ExitStack() as ctx:
        keep = ctx.enter_context(tc.tile_pool(name="keep", bufs=1))
        psum = ctx.enter_context(tc.psum_pool(name="psum", bufs=1))

        list1 = keep.tile([P, J // GROUP], U16, name="list1")
        list2 = keep.tile([P, O // GROUP], U16, name="list2")
        list3 = keep.tile([P, O // GROUP], U16, name="list3")
        list4 = keep.tile([P, O // GROUP], U16, name="list4")
        xt_codes = keep.tile([P, T], I32, name="xt_codes", align_bytes=ALIGN)
        xt_plane = keep.tile([P, T // 4], I32, name="xt_plane", align_bytes=ALIGN)
        w_codes = keep.tile([P, R // 2], I32, name="w_codes", align_bytes=ALIGN)
        w_plane = keep.tile([P, R // 4], I32, name="w_plane", align_bytes=ALIGN)
        wb_codes = keep.tile([P, N], I32, name="wb_codes", align_bytes=ALIGN)
        wb_plane = keep.tile([P, N // 4], I32, name="wb_plane", align_bytes=ALIGN)
        tz_sb = keep.tile([P, N_TILES, Z], F32, name="tz_sb", align_bytes=ALIGN)
        rw_column = keep.tile([P, 1], F32, name="rw_column", align_bytes=ALIGN)
        identity = keep.tile([P, P], F32, name="identity", align_bytes=ALIGN)
        make_identity(nc, identity[:])

        nc.vector.memset(w_plane[:], 0)
        nc.vector.memset(wb_plane[:], 0)

        def load_scale_rows(queue, plane, scales, q):
            rows = scales[0, ROWS * q : ROWS * (q + 1), :].bitcast(I32)
            queue.dma_start(out=plane[QUAD * q : QUAD * q + ROWS, :], in_=rows)

        def load_scale_rows_repeated(queue, plane, scales, q):
            rows = scales[0, ROWS * q : ROWS * (q + 1), :].bitcast(I32)
            repeated = rows.unsqueeze(0).to_broadcast([QUAD // ROWS, ROWS, rows.shape[1]])
            queue.dma_start(out=plane[QUAD * q : QUAD * (q + 1), :], in_=repeated)

        nc.sync.dma_start(list1[:], offs)
        for q in range(QUADS):
            load_scale_rows_repeated((nc.scalar, nc.sync)[q % 2], xt_plane, xt_scales, q)
        nc.scalar.dma_start(out=w_codes[:], in_=w_words[0].bitcast(I32))
        with nc.allow_non_contiguous_dma(reason="one weight a partition"):
            nc.sync.dma_start(out=rw_column[:], in_=rw.rearrange("a o -> o a"))
        nc.scalar.dma_start(out=xt_codes[:], in_=xt_words[0].rearrange("p n t -> p (n t)").bitcast(I32))
        for q in range(QUADS):
            load_scale_rows((nc.sync, nc.scalar)[q % 2], w_plane, w_scales, q)
        nc.sync.dma_start(list2[:], offs2)
        nc.sync.dma_start(list3[:], offs3)
        nc.sync.dma_start(list4[:], offs4)
        nc.sync.dma_start(out=tz_sb[:], in_=tz.rearrange("(h p) z -> p h z", p=P))
        for q in range(QUADS):
            load_scale_rows(nc.sync, wb_plane, wb_scales, q)
        nc.sync.dma_start(out=wb_codes[:], in_=wb_words[0].rearrange("p n t -> p (n t)").bitcast(I32))

        picked_plane = keep.tile([P, J], U8, name="picked_plane", align_bytes=ALIGN)
        picked_codes = keep.tile([P, J], U32, name="picked_codes", align_bytes=ALIGN)
        dealt_codes = keep.tile([P, PACK, P], U16, name="dealt_codes", align_bytes=ALIGN)
        dealt_plane = keep.tile([P, PACK, P], U8, name="dealt_plane", align_bytes=ALIGN)
        nc.vector.tensor_copy(picked_plane[:], xt_plane[:].bitcast(U8).indirect(list1[:]))
        nc.vector.tensor_copy(dealt_codes[:], w_codes[:].bitcast(U16).rearrange("p (q t) -> p t q", t=PACK))
        nc.vector.tensor_copy(picked_codes[:], xt_codes[:].bitcast(U32).indirect(list1[:]))
        w_plane_by_slice = w_plane[:].bitcast(U8).rearrange("p (q t) -> p t q", t=PACK)
        nc.vector.tensor_copy(dealt_plane[:, 0, :], w_plane_by_slice[:, 0, :])
        nc.vector.tensor_copy(dealt_plane[:, 1, :], w_plane_by_slice[:, 1, :])
        nc.vector.tensor_copy(dealt_plane[:, 2:, :], w_plane_by_slice[:, 2:, :])

        a_by_list2 = keep.tile([P, PACK, O], F32, name="a_by_list2", align_bytes=ALIGN)
        a_by_list3 = keep.tile([P, PACK, O], F32, name="a_by_list3", align_bytes=ALIGN)
        a_slices = []
        for t in range(PACK):
            a_bank = psum.tile([P, J], F32, name="a_bank%d" % t, tag="a_bank%d" % t)
            nc.tensor.matmul_mx(
                out=a_bank[:],
                lhsT=dealt_codes[:, t, :].bitcast(E2M1),
                lhsT_scale=dealt_plane[:, t, :],
                rhs=picked_codes[:].bitcast(E5M2),
                rhs_scale=picked_plane[:],
                start=True,
                stop=True,
            )
            a_slice = keep.tile([P, J], F32, name="a_slice%d" % t, tag="a_slice%d" % t, align_bytes=ALIGN)
            if t == 0:
                nc.vector.tensor_copy(a_slice[:], a_bank[:])
            else:
                nc.scalar.activation(a_slice[:], a_bank[:], COPY)
            a_slices.append(a_slice)

        rw_rows = psum.tile([P, O], F32, name="rw_rows", tag="a_bank%d" % (PACK - 1))
        nc.tensor.transpose(rw_rows[:], rw_column[:].to_broadcast([P, P]), identity[:])

        looks = ((a_by_list2, list2), (a_by_list3, list3))
        halves = [(slice(u * HALF, (u + 1) * HALF), slice(u * HALF // GROUP, (u + 1) * HALF // GROUP)) for u in range(2)]
        for t in (0, 1):
            for picked, entries in looks:
                nc.vector.tensor_copy(picked[:, t, :], a_slices[t][:].indirect(entries[:]))
        for places, columns in halves:
            nc.vector.tensor_copy(a_by_list2[:, 2, places], a_slices[2][:].indirect(list2[:, columns]))
        nc.scalar.activation(a_by_list3[:, 2, :], a_slices[2][:].indirect(list3[:]), COPY)
        for places, columns in halves:
            for picked, entries in looks:
                nc.scalar.activation(picked[:, 3, places], a_slices[3][:].indirect(entries[:, columns]), COPY)

        hid = keep.tile([P, O, PACK], BF16, name="hid", align_bytes=ALIGN)
        hid_codes = keep.tile([P, O], U32, name="hid_codes", align_bytes=ALIGN)
        hid_plane = keep.tile([P, O], U8, name="hid_plane", align_bytes=ALIGN)
        for places, columns in halves:
            nc.vector.tensor_tensor(
                hid[:, places, :].rearrange("p (c i) t -> p c t i", i=LINE),
                a_by_list2[:, :, places].rearrange("p t (c i) -> p c t i", i=LINE),
                a_by_list3[:, :, places].rearrange("p t (c i) -> p c t i", i=LINE),
                MAX,
            )
        for places, columns in halves:
            nc.vector.quantize_mx(
                out=hid_codes[:, places].bitcast(E5M2),
                scales=hid_plane[:, places],
                in_=hid[:, places, :].rearrange("p o t -> p (o t)"),
            )

        tz_picked = keep.tile([P, N_TILES, O], F32, name="tz_picked", tag="a_slice%d" % (PACK - 1), align_bytes=ALIGN)
        for h in range(N_TILES):
            nc.scalar.activation(tz_picked[:, h, :], tz_sb[:, h, :].indirect(list4[:]), COPY)

        floored = [keep.tile([P, O], F32, name="floored%d" % h, align_bytes=ALIGN) for h in range(N_TILES)]
        result = [keep.tile([P, O], F32, name="result%d" % h, align_bytes=ALIGN) for h in range(N_TILES)]
        for h in range(N_TILES):
            features = slice(h * P, (h + 1) * P)
            p_bank = psum.tile([P, O], F32, name="p_bank%d" % h)
            nc.tensor.matmul_mx(
                out=p_bank[:],
                lhsT=wb_codes[:, features].bitcast(E4M3),
                lhsT_scale=wb_plane[:].bitcast(U8)[:, features],
                rhs=hid_codes[:].bitcast(E5M2),
                rhs_scale=hid_plane[:],
                start=True,
                stop=True,
            )
            nc.vector.tensor_tensor(floored[h][:], p_bank[:], tz_picked[:, h, :], MAX)
        for h in range(N_TILES):
            nc.vector.tensor_tensor(result[h][:], floored[h][:], rw_rows[:], MULT)
            (nc.sync, nc.scalar)[h].dma_start(out=out[h * P : (h + 1) * P, :], in_=result[h][:])
